import numpy as np
import ml_dtypes


def mxq(x, axis, fmt="e4m3"):
    dtype, down = {"e4m3": (ml_dtypes.float8_e4m3fn, 7), "e5m2": (ml_dtypes.float8_e5m2, 14)}[fmt]
    v = np.moveaxis(np.asarray(x, np.float32).astype(ml_dtypes.bfloat16).astype(np.float64), axis, -1)
    blocks = v.reshape(v.shape[:-1] + (-1, 32))
    amax = np.abs(blocks).max(-1, keepdims=True)
    byte = np.maximum(np.where(amax > 0, np.frexp(amax)[1] - 1 + 127, 0) - down, 1)
    scale = np.exp2(byte - 127.0)
    codes = (blocks / scale).astype(np.float32).astype(dtype).astype(np.float64)
    return np.moveaxis((codes * scale).reshape(v.shape), -1, axis)


WIDE = False


def mx_kscale(k):
    if not WIDE:
        return np.ones(k)
    levels = np.array([10, -10, 5, -5, 0])
    if k % 512:
        return np.exp2(np.random.permutation(np.resize(levels, k // 32))).repeat(32)
    a = np.empty((k // 512, 16))
    for p in range(k // 512):
        a[p, :8] = np.random.permutation(np.resize(levels, 8))
        for g in range(8):
            far = levels[np.abs(levels - a[p, g]) >= 10]
            a[p, g + 8] = far[np.random.randint(len(far))]
    return np.exp2(a.ravel()).repeat(32)


def f64(x):
    return np.asarray(x).astype(np.float64)


def striped(idx):
    return np.tile(idx.reshape(-1, 16).T, (8, 1)).astype(np.uint16)


def unstriped(offs):
    return offs[:16].T.reshape(-1).astype(np.int64)


E2M1 = np.array([0.0, 0.5, 1.0, 1.5, 2.0, 3.0, 4.0, 6.0, -0.0, -0.5, -1.0, -1.5, -2.0, -3.0, -4.0, -6.0])


def pack_weight(w, fmt):
    k, n = w.shape
    w = f64(np.asarray(w, np.float32).astype(ml_dtypes.bfloat16)).reshape(k // 32, 32, n)
    amax = np.abs(w).max(1)
    if fmt == "e4m3":
        byte = np.frexp(amax)[1] - 1 + 127 - 7
    else:
        mant, ex = np.frexp(amax / 6.0)
        byte = np.where(mant > 0.5, ex, ex - 1) + 127
    byte = np.clip(np.where(amax > 0, byte, 1), 1, 254)
    scaled = (w * np.exp2(127.0 - byte)[:, None, :]).reshape(k, n).astype(np.float32)
    by_word = np.ascontiguousarray(scaled.reshape(k // 512, 128, 4, n).transpose(0, 1, 3, 2))
    if fmt == "e4m3":
        words = by_word.astype(ml_dtypes.float8_e4m3fn).view(np.uint8)
    else:
        c = by_word.astype(ml_dtypes.float4_e2m1fn).view(np.uint8) & 0xF
        words = (c[..., 0::2] | (c[..., 1::2] << 4)).reshape(k // 512, 128, 2 * n)
    return np.ascontiguousarray(words), np.ascontiguousarray(byte.astype(np.uint8).reshape(k // 512, 16, n))


def unpack_weight(words, scales, fmt):
    g, _, n = scales.shape
    words = np.ascontiguousarray(words).reshape(g, 128, n, -1)
    if fmt == "e4m3":
        vals = words.view(ml_dtypes.float8_e4m3fn).astype(np.float64)
    else:
        nib = np.empty((g, 128, n, 4), np.uint8)
        nib[..., 0::2] = words & 0xF
        nib[..., 1::2] = words >> 4
        vals = E2M1[nib]
    vals = vals * np.repeat(np.exp2(scales.astype(np.float64) - 127.0), 8, axis=1)[..., None]
    return vals.transpose(0, 1, 3, 2).reshape(g * 512, n)


def gelu(v):
    return 0.5 * v * (1.0 + np.tanh(np.sqrt(2.0 / np.pi) * (v + 0.044715 * v**3)))


K, K2, H, N, S, T, T2 = 1024, 512, 1024, 512, 1024, 4096, 2048

def setup_inputs():
    n = np.random.standard_normal
    s = mx_kscale(K)[:, None]
    s2 = mx_kscale(K2)[:, None]
    u = mx_kscale(H)[:, None]
    tab_words, tab_scales = pack_weight(n((K, T)) * s, "e4m3")
    tab2_words, tab2_scales = pack_weight(n((K2, T2)) * s2, "e4m3")
    ws_words, ws_scales = pack_weight(n((K2, H)) / np.sqrt(K2) / s2, "e2m1")
    return {
        "tab_words": tab_words, "tab_scales": tab_scales,
        "tab2_words": tab2_words, "tab2_scales": tab2_scales,
        "offs": striped(np.random.permutation(T)[:S]),
        "offs2": striped(np.random.permutation(T2)[:S]),
        "wt": (n((K, H)) / np.sqrt(K) / s).astype(np.float32),
        "ws_words": ws_words, "ws_scales": ws_scales,
        "gain": (np.exp(0.2 * n(H)) * u[:, 0]).astype(np.float32),
        "wr": (n((H, N)) / np.sqrt(H) / u).astype(np.float32),
        "br": (0.5 * n(N)).astype(np.float32),
    }

def reference(tab_words, tab_scales, tab2_words, tab2_scales, offs, offs2, wt, ws_words, ws_scales, gain, wr, br):
    v = unpack_weight(tab_words, tab_scales, "e4m3")[:, unstriped(offs)]
    v2 = unpack_weight(tab2_words, tab2_scales, "e4m3")[:, unstriped(offs2)]
    wtq = mxq(f64(wt), 0, "e4m3")
    ws = unpack_weight(ws_words, ws_scales, "e2m1")
    x = wtq.T @ v + ws.T @ v2
    h = np.square(np.maximum(x, 0.0)) * f64(gain)[:, None]
    hq = mxq(h, 0, "e4m3")
    wrq = mxq(f64(wr), 0, "e4m3")
    return (wrq.T @ hq) + f64(br)[:, None]

@@ -1,0 +1,298 @@
+from contextlib import ExitStack
+
+import concourse.mybir as mybir
+from concourse.masks import make_identity
+
+K, K2, H, N, S, T, T2 = 1024, 512, 1024, 512, 1024, 4096, 2048
+FLOPS = 2 * S * (K * H + K2 * H + H * N)
+
+F32 = mybir.dt.float32
+BF16 = mybir.dt.bfloat16
+I32 = mybir.dt.int32
+U32 = mybir.dt.uint32
+U16 = mybir.dt.uint16
+U8 = mybir.dt.uint8
+FP8X4 = mybir.dt.float8_e4m3fn_x4
+FP4X4 = mybir.dt.float4_e2m1fn_x4
+ALU = mybir.AluOpType
+ACT = mybir.ActivationFunctionType
+
+P = 128
+PACK = 4
+KP = 512
+JT = 512
+SQRT_MIN = 2.0 ** -114
+
+
+def tile_list_program_search_ranking_kernel(
+    tc, tab_words, tab_scales, tab2_words, tab2_scales, offs, offs2, wt, ws_words, ws_scales, gain, wr, br, out
+):
+    nc = tc.nc
+    with ExitStack() as ctx:
+        keep = ctx.enter_context(tc.tile_pool(name="keep", bufs=1))
+        psum = ctx.enter_context(tc.psum_pool(name="psum", bufs=8))
+
+        def sb(name, shape, dtype):
+            return keep.tile(shape, dtype, name=name, align_bytes=64)
+
+        list1 = keep.tile([P, S // 16], U16, name="list1")
+        list2 = keep.tile([P, S // 16], U16, name="list2")
+        tab_sc = sb("tab_sc", [P, T // 4], I32)
+        tab2_sc = sb("tab2_sc", [P, T2 // 4], I32)
+        ws_sc_raw = sb("ws_sc_raw", [P, H // 4], I32)
+        nc.vector.memset(tab2_sc[:], 0)
+        nc.vector.memset(tab_sc[:], 0)
+        nc.vector.memset(ws_sc_raw[:], 0)
+
+        tab_w = [sb("tab_w%d" % a, [P, T], I32) for a in range(2)]
+        tab2_w = sb("tab2_w", [P, T2], I32)
+        ws_w_raw = sb("ws_w_raw", [P, H // 2], I32)
+        wt_raw = {(a, b): sb("wt_raw%d%d" % (a, b), [P, PACK, KP], F32) for a in range(2) for b in range(2)}
+        wr_raw = [sb("wr_raw%d" % b, [P, PACK, N], F32) for b in range(2)]
+        vec_rows = sb("vec_rows", [P, P], F32)
+        ident = sb("ident", [P, P], F32)
+        vecs = sb("vecs", [P, 12], F32)
+        nc.vector.memset(vec_rows[:], 0.0)
+        make_identity(nc, ident[:])
+
+        def load_wt(a, b):
+            rows = wt[a * KP : (a + 1) * KP, b * KP : (b + 1) * KP]
+            nc.sync.dma_start(wt_raw[a, b][:], rows.rearrange("(p i) c -> p i c", i=PACK))
+
+        def load_tab(a):
+            nc.sync.dma_start(tab_w[a][:], tab_words[a].rearrange("p t i -> p (t i)").bitcast(I32))
+
+        nc.sync.dma_start(list2[:], offs2)
+        for q in range(4):
+            nc.sync.dma_start(tab2_sc[32 * q : 32 * q + 4, :], tab2_scales[0, 4 * q : 4 * q + 4, :].bitcast(I32))
+        nc.sync.dma_start(list1[:], offs)
+        nc.sync.dma_start(tab2_w[:], tab2_words[0].rearrange("p t i -> p (t i)").bitcast(I32))
+        nc.sync.dma_start(ws_w_raw[:], ws_words[0].bitcast(I32))
+        for q in range(4):
+            nc.sync.dma_start(tab_sc[32 * q + 4 : 32 * q + 12, :], tab_scales[:, 4 * q : 4 * q + 4, :].bitcast(I32))
+        for q in range(4):
+            nc.gpsimd.dma_start(ws_sc_raw[32 * q : 32 * q + 4, :], ws_scales[0, 4 * q : 4 * q + 4, :].bitcast(I32))
+        for b in range(2):
+            nc.gpsimd.dma_start(
+                vec_rows[PACK * b : PACK * (b + 1), :].rearrange("t (B q) -> t B q", q=8),
+                gain[b * KP : (b + 1) * KP].rearrange("(B t q) -> t B q", t=PACK, q=8),
+            )
+        nc.gpsimd.dma_start(vec_rows[8:12, :], br.rearrange("(m p) -> m p", p=P))
+        load_wt(0, 0)
+        load_tab(0)
+        load_wt(1, 0)
+        load_tab(1)
+        load_wt(0, 1)
+        load_wt(1, 1)
+        for b in range(2):
+            rows = wr[b * KP : (b + 1) * KP, :].rearrange("(B t q) n -> t B q n", t=PACK, q=8)
+            for t in range(PACK):
+                nc.sync.dma_start(wr_raw[b][:, t, :], rows[t])
+
+        vecs_ps = psum.tile([P, JT], F32, name="acc")
+        nc.tensor.transpose(vecs_ps[:, :P], vec_rows[:], ident[:])
+        nc.scalar.copy(vecs[:], vecs_ps[:, :12])
+        gf = vecs[:, :8]
+        bias = vecs[:, 8:12]
+        neg = sb("neg", [P, 8], F32)
+        mag = sb("mag", [P, 8], F32)
+        half_root = sb("half_root", [P, 8], F32)
+        inv = sb("inv", [P, 8], F32)
+        corr = sb("corr", [P, 8], F32)
+        root = sb("root", [P, 8], F32)
+        sgn = sb("sgn", [P, 8], F32)
+        nc.vector.tensor_scalar(neg[:], gf, -1.0, SQRT_MIN, ALU.mult, ALU.max)
+        nc.vector.tensor_tensor(mag[:], neg[:], gf, ALU.max)
+        nc.scalar.activation(half_root[:], mag[:], ACT.Sqrt, scale=0.25)
+        nc.scalar.activation(sgn[:], gf, ACT.Sign)
+        nc.vector.reciprocal(inv[:], half_root[:])
+        nc.vector.scalar_tensor_tensor(corr[:], mag[:], 0.25, inv[:], ALU.mult, ALU.mult)
+        nc.vector.tensor_tensor(root[:], corr[:], half_root[:], ALU.add)
+
+        def gather(name, window, dtype, offsets, cols):
+            n = (cols.stop - cols.start) * 16
+            dst = sb(name, [P, n], dtype)
+            nc.vector.tensor_copy(dst[:], window[:].bitcast(dtype).indirect(offsets[:, cols]))
+            return dst
+
+        halves = [slice(0, JT // 16), slice(JT // 16, 2 * JT // 16)]
+        whole = slice(0, S // 16)
+
+        def quantize(name, src, width):
+            codes = sb(name + "_c", [P, width], U32)
+            scales = sb(name + "_s", [P, width], U8)
+            nc.vector.quantize_mx(out=codes[:].bitcast(FP8X4), scales=scales[:], in_=src)
+            return codes, scales
+
+        wt_bf = {}
+        wtq = {}
+
+        def round_wt(a, b, engine):
+            dst = sb("wt_bf%d%d" % (a, b), [P, KP * PACK], BF16)
+            o = dst[:].rearrange("p (t B q i) -> p B t q i", t=PACK, q=8, i=PACK)
+            s = wt_raw[a, b][:].rearrange("p i (B t q) -> p B t q i", t=PACK, q=8)
+            if engine == "scalar":
+                nc.scalar.copy(o, s)
+            else:
+                nc.vector.tensor_copy(o, s)
+            wt_bf[a, b] = dst
+
+        def quant_wt(a, b):
+            wtq[a, b] = quantize("wtq%d%d" % (a, b), wt_bf[a, b][:], KP)
+
+        v2_s = gather("v2_s", tab2_sc, U8, list2, whole)
+        v2_w = [gather("v2_w%d" % j, tab2_w, U32, list2, halves[j]) for j in range(2)]
+        ws_w = sb("ws_w", [P, H // 2], I32)
+        ws_sc = sb("ws_sc", [P, H // 4], I32)
+        for b in range(2):
+            nc.vector.tensor_copy(
+                ws_w[:, b * 256 : (b + 1) * 256].rearrange("p (t B w) -> p B t w", t=PACK, w=4),
+                ws_w_raw[:, b * 256 : (b + 1) * 256].rearrange("p (B t w) -> p B t w", t=PACK, w=4),
+            )
+        v_s = gather("v_s", tab_sc, U8, list1, whole)
+        for b in range(2):
+            nc.vector.tensor_copy(
+                ws_sc[:, b * 128 : (b + 1) * 128].rearrange("p (t B w) -> p B t w", t=PACK, w=2),
+                ws_sc_raw[:, b * 128 : (b + 1) * 128].rearrange("p (B t w) -> p B t w", t=PACK, w=2),
+            )
+        round_wt(0, 0, "scalar")
+        quant_wt(0, 0)
+        v_w = {}
+        for j in range(2):
+            v_w[0, j] = gather("v_w0%d" % j, tab_w[0], U32, list1, halves[j])
+        round_wt(1, 0, "scalar")
+        quant_wt(1, 0)
+
+        x = {}
+
+        def pass_ws(b, j):
+            for t in range(PACK):
+                x[b, j, t] = psum.tile([P, JT], F32, name="acc")
+                c = b * KP + t * P
+                nc.tensor.matmul_mx(
+                    x[b, j, t][:],
+                    lhsT=ws_w[:].bitcast(U8)[:, 2 * c : 2 * (c + P)].bitcast(FP4X4),
+                    lhsT_scale=ws_sc[:].bitcast(U8)[:, c : c + P],
+                    rhs=v2_w[j][:].bitcast(FP8X4),
+                    rhs_scale=v2_s[:, j * JT : (j + 1) * JT],
+                    start=True,
+                    stop=False,
+                )
+
+        def pass_wt(a, b, j):
+            codes, scales = wtq[a, b]
+            for t in range(PACK):
+                nc.tensor.matmul_mx(
+                    x[b, j, t][:],
+                    lhsT=codes[:, t * P : (t + 1) * P].bitcast(FP8X4),
+                    lhsT_scale=scales[:, t * P : (t + 1) * P],
+                    rhs=v_w[a, j][:].bitcast(FP8X4),
+                    rhs_scale=v_s[4 + 4 * a :, j * JT : (j + 1) * JT],
+                    start=False,
+                    stop=(a == 1),
+                )
+
+        r = {}
+        hb = {}
+        hq = {}
+
+        def relu(b, j, engines):
+            r[b, j] = sb("r%d%d" % (b, j), [P, PACK, JT], F32)
+            for t in range(PACK):
+                sc = root[:, b * PACK + t : b * PACK + t + 1]
+                if engines[t] == "s":
+                    nc.scalar.activation(r[b, j][:, t, :], x[b, j, t][:], ACT.Relu, scale=sc)
+                else:
+                    nc.vector.tensor_scalar(r[b, j][:, t, :], x[b, j, t][:], sc, 0.0, ALU.mult, ALU.max)
+
+        def square(b, j, split):
+            hb[b, j] = sb("hb%d%d" % (b, j), [P, JT, PACK], BF16)
+            src = r[b, j][:].rearrange("p t c -> p c t")
+            if split > 0:
+                nc.scalar.activation(hb[b, j][:, :split, :], src[:, :split, :], ACT.Square)
+            if split < JT:
+                nc.vector.tensor_tensor(hb[b, j][:, split:, :], src[:, split:, :], src[:, split:, :], ALU.mult)
+
+        def quant_h(b, j):
+            hq[b, j] = quantize("hq%d%d" % (b, j), hb[b, j][:].rearrange("p c t -> p (c t)"), JT)
+
+        wr_bf = {}
+        wrq = {}
+
+        def round_wr(b):
+            wr_bf[b] = sb("wr_bf%d" % b, [P, N, PACK], BF16)
+            nc.vector.tensor_tensor(
+                wr_bf[b][:],
+                wr_raw[b][:].rearrange("p t n -> p n t"),
+                sgn[:, b * PACK : (b + 1) * PACK].unsqueeze(1).to_broadcast([P, N, PACK]),
+                ALU.mult,
+            )
+
+        def quant_wr(b):
+            wrq[b] = quantize("wrq%d" % b, wr_bf[b][:].rearrange("p n t -> p (n t)"), N)
+
+        y = {}
+
+        def pass_wr(b, j):
+            codes, scales = wrq[b]
+            for m in range(N // P):
+                if b == 0:
+                    y[j, m] = psum.tile([P, JT], F32, name="acc")
+                nc.tensor.matmul_mx(
+                    y[j, m][:],
+                    lhsT=codes[:, m * P : (m + 1) * P].bitcast(FP8X4),
+                    lhsT_scale=scales[:, m * P : (m + 1) * P],
+                    rhs=hq[b, j][0][:].bitcast(FP8X4),
+                    rhs_scale=hq[b, j][1][:],
+                    start=(b == 0),
+                    stop=(b == 1),
+                )
+
+        def finish(j, engines):
+            for m in range(N // P):
+                res = sb("res%d%d" % (j, m), [P, JT], F32)
+                if engines[m] == "s":
+                    nc.scalar.activation(res[:], y[j, m][:], ACT.Identity, bias=bias[:, m : m + 1])
+                else:
+                    nc.vector.tensor_scalar(res[:], y[j, m][:], bias[:, m : m + 1], None, ALU.add)
+                nc.sync.dma_start(out[m * P : (m + 1) * P, j * JT : (j + 1) * JT], res[:])
+
+        pass_ws(0, 0)
+        pass_ws(0, 1)
+        pass_wt(0, 0, 0)
+        pass_wt(0, 0, 1)
+        for j in range(2):
+            v_w[1, j] = gather("v_w1%d" % j, tab_w[1], U32, list1, halves[j])
+            pass_wt(1, 0, j)
+        relu(0, 0, "ssss")
+        round_wt(0, 1, "vector")
+        relu(0, 1, "ssss")
+        quant_wt(0, 1)
+        round_wt(1, 1, "vector")
+        pass_ws(1, 0)
+        pass_wt(0, 1, 0)
+        square(0, 0, 256)
+        quant_wt(1, 1)
+        pass_ws(1, 1)
+        pass_wt(1, 1, 0)
+        pass_wt(0, 1, 1)
+        pass_wt(1, 1, 1)
+        square(0, 1, 512)
+        quant_h(0, 0)
+        round_wr(0)
+        relu(1, 0, "ssss")
+        quant_wr(0)
+        quant_h(0, 1)
+        round_wr(1)
+        relu(1, 1, "ssss")
+        quant_wr(1)
+        pass_wr(0, 0)
+        square(1, 0, 256)
+        quant_h(1, 0)
+        pass_wr(0, 1)
+        pass_wr(1, 0)
+        square(1, 1, 256)
+        quant_h(1, 1)
+        finish(0, "svsv")
+        pass_wr(1, 1)
+        finish(1, "svsv")

@@ -30,6 +30,7 @@ def tile_list_program_search_ranking_kernel(
     nc = tc.nc
     with ExitStack() as ctx:
         keep = ctx.enter_context(tc.tile_pool(name="keep", bufs=1))
+        reuse = ctx.enter_context(tc.tile_pool(name="reuse", bufs=1))
         psum = ctx.enter_context(tc.psum_pool(name="psum", bufs=8))
 
         def sb(name, shape, dtype):
@@ -40,48 +41,61 @@ def tile_list_program_search_ranking_kernel(
         tab_sc = sb("tab_sc", [P, T // 4], I32)
         tab2_sc = sb("tab2_sc", [P, T2 // 4], I32)
         ws_sc_raw = sb("ws_sc_raw", [P, H // 4], I32)
+        gain_rows = sb("gain_rows", [P, 2 * P], F32)
+        nc.vector.memset(gain_rows[:], 0.0)
         nc.vector.memset(tab2_sc[:], 0)
-        nc.vector.memset(tab_sc[:], 0)
         nc.vector.memset(ws_sc_raw[:], 0)
+        nc.vector.memset(tab_sc[:], 0)
 
-        tab_w = [sb("tab_w%d" % a, [P, T], I32) for a in range(2)]
+        tab_w = [sb("tab_w0", [P, T], I32), reuse.tile([P, T], I32, name="tab_w1", align_bytes=64, offset=0)]
+
+        def late_bf16(name, shape, slot):
+            return reuse.tile(shape, BF16, name=name, align_bytes=64, offset=slot * 4096)
+
         tab2_w = sb("tab2_w", [P, T2], I32)
         ws_w_raw = sb("ws_w_raw", [P, H // 2], I32)
         wt_raw = {(a, b): sb("wt_raw%d%d" % (a, b), [P, PACK, KP], F32) for a in range(2) for b in range(2)}
         wr_raw = [sb("wr_raw%d" % b, [P, PACK, N], F32) for b in range(2)]
-        vec_rows = sb("vec_rows", [P, P], F32)
+        bias = sb("bias", [P, N // P], F32)
         ident = sb("ident", [P, P], F32)
-        vecs = sb("vecs", [P, 12], F32)
-        nc.vector.memset(vec_rows[:], 0.0)
+        vecs = sb("vecs", [P, 2, PACK], F32)
         make_identity(nc, ident[:])
 
-        def load_wt(a, b):
-            rows = wt[a * KP : (a + 1) * KP, b * KP : (b + 1) * KP]
-            nc.sync.dma_start(wt_raw[a, b][:], rows.rearrange("(p i) c -> p i c", i=PACK))
+        def load_wt(a, b, half=None):
+            rows = wt[a * KP : (a + 1) * KP, b * KP : (b + 1) * KP].rearrange("(p i) c -> p i c", i=PACK)
+            slots = slice(0, PACK) if half is None else slice(2 * half, 2 * half + 2)
+            nc.sync.dma_start(wt_raw[a, b][:, slots, :], rows[:, slots, :])
 
         def load_tab(a):
             nc.sync.dma_start(tab_w[a][:], tab_words[a].rearrange("p t i -> p (t i)").bitcast(I32))
 
+        def load_rows(dst, src, first, q):
+            nc.sync.dma_start(dst[32 * q + first : 32 * q + first + 4, :], src[4 * q : 4 * q + 4, :].bitcast(I32))
+
         nc.sync.dma_start(list2[:], offs2)
-        for q in range(4):
-            nc.sync.dma_start(tab2_sc[32 * q : 32 * q + 4, :], tab2_scales[0, 4 * q : 4 * q + 4, :].bitcast(I32))
         nc.sync.dma_start(list1[:], offs)
-        nc.sync.dma_start(tab2_w[:], tab2_words[0].rearrange("p t i -> p (t i)").bitcast(I32))
+        tab2_hbm = tab2_words[0].rearrange("p t i -> p (t i)").bitcast(I32)
+        for c in range(0, T2, 512):
+            nc.sync.dma_start(tab2_w[:, c : c + 512], tab2_hbm[:, c : c + 512])
         nc.sync.dma_start(ws_w_raw[:], ws_words[0].bitcast(I32))
+        load_wt(0, 0, 0)
+        nc.sync.dma_start(
+            gain_rows[:PACK, :].rearrange("t (B q) -> t B q", q=8),
+            gain.rearrange("(B t q) -> t B q", t=PACK, q=8),
+        )
+        for q in range(4):
+            load_rows(tab2_sc, tab2_scales[0], 0, q)
+        load_wt(0, 0, 1)
+        for q in range(4):
+            load_rows(ws_sc_raw, ws_scales[0], 0, q)
+        load_wt(1, 0, 0)
         for q in range(4):
             nc.sync.dma_start(tab_sc[32 * q + 4 : 32 * q + 12, :], tab_scales[:, 4 * q : 4 * q + 4, :].bitcast(I32))
-        for q in range(4):
-            nc.gpsimd.dma_start(ws_sc_raw[32 * q : 32 * q + 4, :], ws_scales[0, 4 * q : 4 * q + 4, :].bitcast(I32))
-        for b in range(2):
-            nc.gpsimd.dma_start(
-                vec_rows[PACK * b : PACK * (b + 1), :].rearrange("t (B q) -> t B q", q=8),
-                gain[b * KP : (b + 1) * KP].rearrange("(B t q) -> t B q", t=PACK, q=8),
-            )
-        nc.gpsimd.dma_start(vec_rows[8:12, :], br.rearrange("(m p) -> m p", p=P))
-        load_wt(0, 0)
+        load_wt(1, 0, 1)
         load_tab(0)
-        load_wt(1, 0)
         load_tab(1)
+        with nc.allow_non_contiguous_dma(reason="one bias value a partition"):
+            nc.sync.dma_start(bias[:], br.rearrange("(m p) -> p m", p=P))
         load_wt(0, 1)
         load_wt(1, 1)
         for b in range(2):
@@ -90,10 +104,10 @@ def tile_list_program_search_ranking_kernel(
                 nc.sync.dma_start(wr_raw[b][:, t, :], rows[t])
 
         vecs_ps = psum.tile([P, JT], F32, name="acc")
-        nc.tensor.transpose(vecs_ps[:, :P], vec_rows[:], ident[:])
-        nc.scalar.copy(vecs[:], vecs_ps[:, :12])
-        gf = vecs[:, :8]
-        bias = vecs[:, 8:12]
+        for b in range(2):
+            nc.tensor.transpose(vecs_ps[:, b * P : (b + 1) * P], gain_rows[:, b * P : (b + 1) * P], ident[:])
+        nc.vector.tensor_copy(vecs[:], vecs_ps[:, : 2 * P].rearrange("p (b c) -> p b c", b=2)[:, :, :PACK])
+        gf = vecs[:].rearrange("p b t -> p (b t)")
         neg = sb("neg", [P, 8], F32)
         mag = sb("mag", [P, 8], F32)
         half_root = sb("half_root", [P, 8], F32)
@@ -128,19 +142,22 @@ def tile_list_program_search_ranking_kernel(
         wtq = {}
 
         def round_wt(a, b, engine):
-            dst = sb("wt_bf%d%d" % (a, b), [P, KP * PACK], BF16)
-            o = dst[:].rearrange("p (t B q i) -> p B t q i", t=PACK, q=8, i=PACK)
-            s = wt_raw[a, b][:].rearrange("p i (B t q) -> p B t q i", t=PACK, q=8)
-            if engine == "scalar":
-                nc.scalar.copy(o, s)
+            if b == 0:
+                dst = sb("wt_bf%d%d" % (a, b), [P, KP * PACK], BF16)
             else:
-                nc.vector.tensor_copy(o, s)
+                dst = late_bf16("wt_bf%d%d" % (a, b), [P, KP * PACK], 0)
+            o = dst[:].rearrange("p (t B q i) -> p t B i q", t=PACK, q=8, i=PACK)
+            s = wt_raw[a, b][:].rearrange("p i (B t q) -> p t B i q", t=PACK, q=8)
+            for t in range(PACK):
+                if engine[t] == "s":
+                    nc.scalar.copy(o[:, t], s[:, t])
+                else:
+                    nc.vector.tensor_copy(o[:, t], s[:, t])
             wt_bf[a, b] = dst
 
         def quant_wt(a, b):
             wtq[a, b] = quantize("wtq%d%d" % (a, b), wt_bf[a, b][:], KP)
 
-        v2_s = gather("v2_s", tab2_sc, U8, list2, whole)
         v2_w = [gather("v2_w%d" % j, tab2_w, U32, list2, halves[j]) for j in range(2)]
         ws_w = sb("ws_w", [P, H // 2], I32)
         ws_sc = sb("ws_sc", [P, H // 4], I32)
@@ -149,19 +166,20 @@ def tile_list_program_search_ranking_kernel(
                 ws_w[:, b * 256 : (b + 1) * 256].rearrange("p (t B w) -> p B t w", t=PACK, w=4),
                 ws_w_raw[:, b * 256 : (b + 1) * 256].rearrange("p (B t w) -> p B t w", t=PACK, w=4),
             )
-        v_s = gather("v_s", tab_sc, U8, list1, whole)
+        v2_s = gather("v2_s", tab2_sc, U8, list2, whole)
         for b in range(2):
             nc.vector.tensor_copy(
                 ws_sc[:, b * 128 : (b + 1) * 128].rearrange("p (t B w) -> p B t w", t=PACK, w=2),
                 ws_sc_raw[:, b * 128 : (b + 1) * 128].rearrange("p (B t w) -> p B t w", t=PACK, w=2),
             )
-        round_wt(0, 0, "scalar")
+        v_s = gather("v_s", tab_sc, U8, list1, whole)
+        round_wt(0, 0, "ssss")
+        round_wt(1, 0, "ssss")
         quant_wt(0, 0)
+        quant_wt(1, 0)
         v_w = {}
         for j in range(2):
             v_w[0, j] = gather("v_w0%d" % j, tab_w[0], U32, list1, halves[j])
-        round_wt(1, 0, "scalar")
-        quant_wt(1, 0)
 
         x = {}
 
@@ -196,22 +214,24 @@ def tile_list_program_search_ranking_kernel(
         hb = {}
         hq = {}
 
-        def relu(b, j, engines):
-            r[b, j] = sb("r%d%d" % (b, j), [P, PACK, JT], F32)
-            for t in range(PACK):
-                sc = root[:, b * PACK + t : b * PACK + t + 1]
-                if engines[t] == "s":
-                    nc.scalar.activation(r[b, j][:, t, :], x[b, j, t][:], ACT.Relu, scale=sc)
-                else:
-                    nc.vector.tensor_scalar(r[b, j][:, t, :], x[b, j, t][:], sc, 0.0, ALU.mult, ALU.max)
+        def relu(b, j, t, engine):
+            if (b, j) not in r:
+                r[b, j] = sb("r%d%d" % (b, j), [P, PACK, JT], F32)
+            sc = root[:, b * PACK + t : b * PACK + t + 1]
+            if engine == "s":
+                nc.scalar.activation(r[b, j][:, t, :], x[b, j, t][:], ACT.Relu, scale=sc)
+            else:
+                nc.vector.tensor_scalar(r[b, j][:, t, :], x[b, j, t][:], sc, 0.0, ALU.mult, ALU.max)
 
-        def square(b, j, split):
-            hb[b, j] = sb("hb%d%d" % (b, j), [P, JT, PACK], BF16)
-            src = r[b, j][:].rearrange("p t c -> p c t")
-            if split > 0:
-                nc.scalar.activation(hb[b, j][:, :split, :], src[:, :split, :], ACT.Square)
-            if split < JT:
-                nc.vector.tensor_tensor(hb[b, j][:, split:, :], src[:, split:, :], src[:, split:, :], ALU.mult)
+        def square(b, j, engine, lo, hi):
+            if (b, j) not in hb:
+                hb[b, j] = sb("hb%d%d" % (b, j), [P, JT, PACK], BF16)
+            src = r[b, j][:, :, lo:hi].rearrange("p t (c i) -> p c t i", i=4)
+            dst = hb[b, j][:, lo:hi, :].rearrange("p (c i) t -> p c t i", i=4)
+            if engine == "s":
+                nc.scalar.activation(dst, src, ACT.Square)
+            else:
+                nc.vector.tensor_tensor(dst, src, src, ALU.mult)
 
         def quant_h(b, j):
             hq[b, j] = quantize("hq%d%d" % (b, j), hb[b, j][:].rearrange("p c t -> p (c t)"), JT)
@@ -219,12 +239,13 @@ def tile_list_program_search_ranking_kernel(
         wr_bf = {}
         wrq = {}
 
-        def round_wr(b):
-            wr_bf[b] = sb("wr_bf%d" % b, [P, N, PACK], BF16)
+        def round_wr(b, lo, hi):
+            if b not in wr_bf:
+                wr_bf[b] = late_bf16("wr_bf%d" % b, [P, N, PACK], 0)
             nc.vector.tensor_tensor(
-                wr_bf[b][:],
-                wr_raw[b][:].rearrange("p t n -> p n t"),
-                sgn[:, b * PACK : (b + 1) * PACK].unsqueeze(1).to_broadcast([P, N, PACK]),
+                wr_bf[b][:, lo:hi, :].rearrange("p (c i) t -> p c t i", i=4),
+                wr_raw[b][:, :, lo:hi].rearrange("p t (c i) -> p c t i", i=4),
+                sgn[:, b * PACK : (b + 1) * PACK].unsqueeze(1).unsqueeze(3).to_broadcast([P, (hi - lo) // 4, PACK, 4]),
                 ALU.mult,
             )
 
@@ -248,14 +269,13 @@ def tile_list_program_search_ranking_kernel(
                     stop=(b == 1),
                 )
 
-        def finish(j, engines):
-            for m in range(N // P):
-                res = sb("res%d%d" % (j, m), [P, JT], F32)
-                if engines[m] == "s":
-                    nc.scalar.activation(res[:], y[j, m][:], ACT.Identity, bias=bias[:, m : m + 1])
-                else:
-                    nc.vector.tensor_scalar(res[:], y[j, m][:], bias[:, m : m + 1], None, ALU.add)
-                nc.sync.dma_start(out[m * P : (m + 1) * P, j * JT : (j + 1) * JT], res[:])
+        def finish(j, m, engine):
+            res = sb("res%d%d" % (j, m), [P, JT], F32)
+            if engine == "s":
+                nc.scalar.activation(res[:], y[j, m][:], ACT.Identity, bias=bias[:, m : m + 1])
+            else:
+                nc.vector.tensor_scalar(res[:], y[j, m][:], bias[:, m : m + 1], None, ALU.add)
+            nc.sync.dma_start(out[m * P : (m + 1) * P, j * JT : (j + 1) * JT], res[:])
 
         pass_ws(0, 0)
         pass_ws(0, 1)
@@ -264,35 +284,59 @@ def tile_list_program_search_ranking_kernel(
         for j in range(2):
             v_w[1, j] = gather("v_w1%d" % j, tab_w[1], U32, list1, halves[j])
             pass_wt(1, 0, j)
-        relu(0, 0, "ssss")
-        round_wt(0, 1, "vector")
-        relu(0, 1, "ssss")
-        quant_wt(0, 1)
-        round_wt(1, 1, "vector")
+        relu(0, 0, 0, "s")
+        relu(0, 0, 1, "s")
+        relu(0, 0, 2, "s")
+        relu(0, 1, 0, "s")
+        relu(0, 0, 3, "s")
+        round_wt(0, 1, "vvvv")
         pass_ws(1, 0)
+        relu(0, 1, 2, "s")
+        quant_wt(0, 1)
         pass_wt(0, 1, 0)
-        square(0, 0, 256)
-        quant_wt(1, 1)
+        relu(0, 1, 1, "s")
+        round_wt(1, 1, "vvvv")
+        relu(0, 1, 3, "s")
         pass_ws(1, 1)
-        pass_wt(1, 1, 0)
         pass_wt(0, 1, 1)
+        square(0, 0, "s", 256, 512)
+        round_wr(0, 256, 512)
+        round_wr(0, 0, 256)
+        quant_wt(1, 1)
+        pass_wt(1, 1, 0)
+        relu(1, 0, 0, "s")
         pass_wt(1, 1, 1)
-        square(0, 1, 512)
-        quant_h(0, 0)
-        round_wr(0)
-        relu(1, 0, "ssss")
+        relu(1, 0, 1, "s")
+        relu(1, 0, 2, "s")
+        square(0, 0, "s", 0, 256)
         quant_wr(0)
-        quant_h(0, 1)
-        round_wr(1)
-        relu(1, 1, "ssss")
-        quant_wr(1)
+        relu(1, 1, 1, "s")
+        quant_h(0, 0)
+        round_wr(1, 256, 512)
+        round_wr(1, 0, 256)
+        relu(1, 0, 3, "s")
+        square(1, 0, "s", 0, 256)
+        relu(1, 1, 2, "v")
         pass_wr(0, 0)
-        square(1, 0, 256)
+        relu(1, 1, 0, "s")
+        square(1, 0, "s", 256, 512)
+        relu(1, 1, 3, "s")
         quant_h(1, 0)
-        pass_wr(0, 1)
+        quant_wr(1)
+        square(1, 1, "v", 256, 512)
         pass_wr(1, 0)
-        square(1, 1, 256)
+        square(0, 1, "s", 256, 512)
+        square(0, 1, "s", 0, 256)
+        square(1, 1, "v", 0, 256)
+        quant_h(0, 1)
+        pass_wr(0, 1)
         quant_h(1, 1)
-        finish(0, "svsv")
+        finish(0, 1, "v")
         pass_wr(1, 1)
-        finish(1, "svsv")
+        finish(0, 3, "s")
+        finish(0, 2, "s")
+        finish(1, 3, "s")
+        finish(0, 0, "s")
+        finish(1, 0, "s")
+        finish(1, 1, "v")
+        finish(1, 2, "v")

@@ -38,14 +38,14 @@ def tile_list_program_search_ranking_kernel(
 
         list1 = keep.tile([P, S // 16], U16, name="list1")
         list2 = keep.tile([P, S // 16], U16, name="list2")
-        tab_sc = sb("tab_sc", [P, T // 4], I32)
+        tab_sc = reuse.tile([P, T // 4], I32, name="tab_sc", align_bytes=64, offset=4 * T)
         tab2_sc = sb("tab2_sc", [P, T2 // 4], I32)
         ws_sc_raw = sb("ws_sc_raw", [P, H // 4], I32)
         gain_rows = sb("gain_rows", [P, 2 * P], F32)
+        nc.vector.memset(tab_sc[:], 0)
         nc.vector.memset(gain_rows[:], 0.0)
         nc.vector.memset(tab2_sc[:], 0)
         nc.vector.memset(ws_sc_raw[:], 0)
-        nc.vector.memset(tab_sc[:], 0)
 
         tab_w = [sb("tab_w0", [P, T], I32), reuse.tile([P, T], I32, name="tab_w1", align_bytes=64, offset=0)]
 
@@ -69,9 +69,12 @@ def tile_list_program_search_ranking_kernel(
         def load_tab(a):
             nc.sync.dma_start(tab_w[a][:], tab_words[a].rearrange("p t i -> p (t i)").bitcast(I32))
 
-        def load_rows(dst, src, first, q):
-            nc.sync.dma_start(dst[32 * q + first : 32 * q + first + 4, :], src[4 * q : 4 * q + 4, :].bitcast(I32))
+        def load_rows(dst, src):
+            for k in range(4):
+                nc.sync.dma_start(dst[k:P:32, :], src[k:16:4, :].bitcast(I32))
 
+        for q in range(4):
+            nc.gpsimd.dma_start(tab_sc[32 * q + 4 : 32 * q + 12, :], tab_scales[:, 4 * q : 4 * q + 4, :].bitcast(I32))
         nc.sync.dma_start(list2[:], offs2)
         nc.sync.dma_start(list1[:], offs)
         tab2_hbm = tab2_words[0].rearrange("p t i -> p (t i)").bitcast(I32)
@@ -83,15 +86,10 @@ def tile_list_program_search_ranking_kernel(
             gain_rows[:PACK, :].rearrange("t (B q) -> t B q", q=8),
             gain.rearrange("(B t q) -> t B q", t=PACK, q=8),
         )
-        for q in range(4):
-            load_rows(tab2_sc, tab2_scales[0], 0, q)
+        load_rows(tab2_sc, tab2_scales[0])
         load_wt(0, 0, 1)
-        for q in range(4):
-            load_rows(ws_sc_raw, ws_scales[0], 0, q)
-        load_wt(1, 0, 0)
-        for q in range(4):
-            nc.sync.dma_start(tab_sc[32 * q + 4 : 32 * q + 12, :], tab_scales[:, 4 * q : 4 * q + 4, :].bitcast(I32))
-        load_wt(1, 0, 1)
+        load_rows(ws_sc_raw, ws_scales[0])
+        load_wt(1, 0)
         load_tab(0)
         load_tab(1)
         with nc.allow_non_contiguous_dma(reason="one bias value a partition"):
@@ -123,9 +121,12 @@ def tile_list_program_search_ranking_kernel(
         nc.vector.scalar_tensor_tensor(corr[:], mag[:], 0.25, inv[:], ALU.mult, ALU.mult)
         nc.vector.tensor_tensor(root[:], corr[:], half_root[:], ALU.add)
 
-        def gather(name, window, dtype, offsets, cols):
+        def gather(name, window, dtype, offsets, cols, offset=None):
             n = (cols.stop - cols.start) * 16
-            dst = sb(name, [P, n], dtype)
+            if offset is None:
+                dst = sb(name, [P, n], dtype)
+            else:
+                dst = reuse.tile([P, n], dtype, name=name, align_bytes=64, offset=offset)
             nc.vector.tensor_copy(dst[:], window[:].bitcast(dtype).indirect(offsets[:, cols]))
             return dst
 
@@ -146,13 +147,12 @@ def tile_list_program_search_ranking_kernel(
                 dst = sb("wt_bf%d%d" % (a, b), [P, KP * PACK], BF16)
             else:
                 dst = late_bf16("wt_bf%d%d" % (a, b), [P, KP * PACK], 0)
-            o = dst[:].rearrange("p (t B q i) -> p t B i q", t=PACK, q=8, i=PACK)
-            s = wt_raw[a, b][:].rearrange("p i (B t q) -> p t B i q", t=PACK, q=8)
-            for t in range(PACK):
-                if engine[t] == "s":
-                    nc.scalar.copy(o[:, t], s[:, t])
-                else:
-                    nc.vector.tensor_copy(o[:, t], s[:, t])
+            o = dst[:].rearrange("p (t B q i) -> p B t q i", t=PACK, q=8, i=PACK)
+            s = wt_raw[a, b][:].rearrange("p i (B t q) -> p B t q i", t=PACK, q=8)
+            if engine[0] == "s":
+                nc.scalar.copy(o, s)
+            else:
+                nc.vector.tensor_copy(o, s)
             wt_bf[a, b] = dst
 
         def quant_wt(a, b):
@@ -179,7 +179,7 @@ def tile_list_program_search_ranking_kernel(
         quant_wt(1, 0)
         v_w = {}
         for j in range(2):
-            v_w[0, j] = gather("v_w0%d" % j, tab_w[0], U32, list1, halves[j])
+            v_w[0, j] = gather("v_w0%d" % j, tab_w[0], U32, list1, halves[j], 4 * T + 4 * JT * j)
 
         x = {}
 
@@ -226,8 +226,8 @@ def tile_list_program_search_ranking_kernel(
         def square(b, j, engine, lo, hi):
             if (b, j) not in hb:
                 hb[b, j] = sb("hb%d%d" % (b, j), [P, JT, PACK], BF16)
-            src = r[b, j][:, :, lo:hi].rearrange("p t (c i) -> p c t i", i=4)
-            dst = hb[b, j][:, lo:hi, :].rearrange("p (c i) t -> p c t i", i=4)
+            src = r[b, j][:, :, lo:hi].rearrange("p t c -> p c t")
+            dst = hb[b, j][:, lo:hi, :]
             if engine == "s":
                 nc.scalar.activation(dst, src, ACT.Square)
             else:
@@ -243,9 +243,9 @@ def tile_list_program_search_ranking_kernel(
             if b not in wr_bf:
                 wr_bf[b] = late_bf16("wr_bf%d" % b, [P, N, PACK], 0)
             nc.vector.tensor_tensor(
-                wr_bf[b][:, lo:hi, :].rearrange("p (c i) t -> p c t i", i=4),
-                wr_raw[b][:, :, lo:hi].rearrange("p t (c i) -> p c t i", i=4),
-                sgn[:, b * PACK : (b + 1) * PACK].unsqueeze(1).unsqueeze(3).to_broadcast([P, (hi - lo) // 4, PACK, 4]),
+                wr_bf[b][:, lo:hi, :],
+                wr_raw[b][:, :, lo:hi].rearrange("p t c -> p c t"),
+                sgn[:, b * PACK : (b + 1) * PACK].unsqueeze(1).to_broadcast([P, hi - lo, PACK]),
                 ALU.mult,
             )
 
@@ -287,56 +287,56 @@ def tile_list_program_search_ranking_kernel(
         relu(0, 0, 0, "s")
         relu(0, 0, 1, "s")
         relu(0, 0, 2, "s")
-        relu(0, 1, 0, "s")
         relu(0, 0, 3, "s")
         round_wt(0, 1, "vvvv")
-        pass_ws(1, 0)
-        relu(0, 1, 2, "s")
-        quant_wt(0, 1)
-        pass_wt(0, 1, 0)
+        relu(0, 1, 0, "s")
         relu(0, 1, 1, "s")
+        relu(0, 1, 2, "s")
+        relu(0, 1, 3, "v")
+        quant_wt(0, 1)
+        pass_ws(1, 0)
+        pass_wt(0, 1, 0)
         round_wt(1, 1, "vvvv")
-        relu(0, 1, 3, "s")
         pass_ws(1, 1)
         pass_wt(0, 1, 1)
-        square(0, 0, "s", 256, 512)
-        round_wr(0, 256, 512)
-        round_wr(0, 0, 256)
         quant_wt(1, 1)
         pass_wt(1, 1, 0)
-        relu(1, 0, 0, "s")
         pass_wt(1, 1, 1)
+        square(0, 0, "s", 0, 256)
+        square(0, 0, "s", 256, 512)
+        round_wr(0, 0, 256)
+        round_wr(0, 256, 512)
+        relu(1, 0, 0, "s")
         relu(1, 0, 1, "s")
         relu(1, 0, 2, "s")
-        square(0, 0, "s", 0, 256)
-        quant_wr(0)
-        relu(1, 1, 1, "s")
-        quant_h(0, 0)
-        round_wr(1, 256, 512)
-        round_wr(1, 0, 256)
         relu(1, 0, 3, "s")
-        square(1, 0, "s", 0, 256)
-        relu(1, 1, 2, "v")
+        quant_h(0, 0)
+        quant_wr(0)
         pass_wr(0, 0)
-        relu(1, 1, 0, "s")
+        round_wr(1, 0, 256)
+        round_wr(1, 256, 512)
+        square(1, 0, "s", 0, 256)
         square(1, 0, "s", 256, 512)
-        relu(1, 1, 3, "s")
-        quant_h(1, 0)
         quant_wr(1)
-        square(1, 1, "v", 256, 512)
+        quant_h(1, 0)
         pass_wr(1, 0)
+        relu(1, 1, 0, "s")
+        relu(1, 1, 1, "s")
+        relu(1, 1, 2, "s")
+        relu(1, 1, 3, "s")
+        square(0, 1, "v", 0, 256)
         square(0, 1, "s", 256, 512)
-        square(0, 1, "s", 0, 256)
-        square(1, 1, "v", 0, 256)
         quant_h(0, 1)
         pass_wr(0, 1)
+        square(1, 1, "s", 0, 256)
+        square(1, 1, "v", 256, 512)
         quant_h(1, 1)
+        finish(0, 0, "v")
         finish(0, 1, "v")
-        pass_wr(1, 1)
-        finish(0, 3, "s")
         finish(0, 2, "s")
-        finish(1, 3, "s")
-        finish(0, 0, "s")
-        finish(1, 0, "s")
-        finish(1, 1, "v")
+        finish(0, 3, "s")
+        pass_wr(1, 1)
+        finish(1, 0, "v")
+        finish(1, 1, "s")
         finish(1, 2, "v")
+        finish(1, 3, "s")

from contextlib import ExitStack

import concourse.mybir as mybir
from concourse.masks import make_identity

K, K2, H, N, S, T, T2 = 1024, 512, 1024, 512, 1024, 4096, 2048
FLOPS = 2 * S * (K * H + K2 * H + H * N)

F32 = mybir.dt.float32
BF16 = mybir.dt.bfloat16
I32 = mybir.dt.int32
U32 = mybir.dt.uint32
U16 = mybir.dt.uint16
U8 = mybir.dt.uint8
FP8X4 = mybir.dt.float8_e4m3fn_x4
FP4X4 = mybir.dt.float4_e2m1fn_x4
ALU = mybir.AluOpType
ACT = mybir.ActivationFunctionType

P = 128
PACK = 4
KP = 512
JT = 512
SQRT_MIN = 2.0 ** -114


def tile_list_program_search_ranking_kernel(
    tc, tab_words, tab_scales, tab2_words, tab2_scales, offs, offs2, wt, ws_words, ws_scales, gain, wr, br, out
):
    nc = tc.nc
    with ExitStack() as ctx:
        keep = ctx.enter_context(tc.tile_pool(name="keep", bufs=1))
        reuse = ctx.enter_context(tc.tile_pool(name="reuse", bufs=1))
        psum = ctx.enter_context(tc.psum_pool(name="psum", bufs=8))

        def sb(name, shape, dtype):
            return keep.tile(shape, dtype, name=name, align_bytes=64)

        list1 = keep.tile([P, S // 16], U16, name="list1")
        list2 = keep.tile([P, S // 16], U16, name="list2")
        tab_sc = reuse.tile([P, T // 4], I32, name="tab_sc", align_bytes=64, offset=4 * T)
        tab2_sc = sb("tab2_sc", [P, T2 // 4], I32)
        ws_sc_raw = sb("ws_sc_raw", [P, H // 4], I32)
        gain_rows = sb("gain_rows", [P, 2 * P], F32)
        nc.vector.memset(tab_sc[:], 0)
        nc.vector.memset(gain_rows[:], 0.0)
        nc.vector.memset(tab2_sc[:], 0)
        nc.vector.memset(ws_sc_raw[:], 0)

        tab_w = [sb("tab_w0", [P, T], I32), reuse.tile([P, T], I32, name="tab_w1", align_bytes=64, offset=0)]

        def late_bf16(name, shape, slot):
            return reuse.tile(shape, BF16, name=name, align_bytes=64, offset=slot * 4096)

        tab2_w = sb("tab2_w", [P, T2], I32)
        ws_w_raw = sb("ws_w_raw", [P, H // 2], I32)
        wt_raw = {(a, b): sb("wt_raw%d%d" % (a, b), [P, PACK, KP], F32) for a in range(2) for b in range(2)}
        wr_raw = [sb("wr_raw%d" % b, [P, PACK, N], F32) for b in range(2)]
        bias = sb("bias", [P, N // P], F32)
        ident = sb("ident", [P, P], F32)
        vecs = sb("vecs", [P, 2, PACK], F32)
        make_identity(nc, ident[:])

        def load_wt(a, b, half=None):
            rows = wt[a * KP : (a + 1) * KP, b * KP : (b + 1) * KP].rearrange("(p i) c -> p i c", i=PACK)
            slots = slice(0, PACK) if half is None else slice(2 * half, 2 * half + 2)
            nc.sync.dma_start(wt_raw[a, b][:, slots, :], rows[:, slots, :])

        def load_tab(a):
            nc.sync.dma_start(tab_w[a][:], tab_words[a].rearrange("p t i -> p (t i)").bitcast(I32))

        def load_rows(dst, src):
            for k in range(4):
                nc.sync.dma_start(dst[k:P:32, :], src[k:16:4, :].bitcast(I32))

        for q in range(4):
            nc.gpsimd.dma_start(tab_sc[32 * q + 4 : 32 * q + 12, :], tab_scales[:, 4 * q : 4 * q + 4, :].bitcast(I32))
        nc.sync.dma_start(list2[:], offs2)
        nc.sync.dma_start(list1[:], offs)
        tab2_hbm = tab2_words[0].rearrange("p t i -> p (t i)").bitcast(I32)
        for c in range(0, T2, 512):
            nc.sync.dma_start(tab2_w[:, c : c + 512], tab2_hbm[:, c : c + 512])
        nc.sync.dma_start(ws_w_raw[:], ws_words[0].bitcast(I32))
        load_wt(0, 0, 0)
        nc.sync.dma_start(
            gain_rows[:PACK, :].rearrange("t (B q) -> t B q", q=8),
            gain.rearrange("(B t q) -> t B q", t=PACK, q=8),
        )
        load_rows(tab2_sc, tab2_scales[0])
        load_wt(0, 0, 1)
        load_rows(ws_sc_raw, ws_scales[0])
        load_wt(1, 0)
        load_tab(0)
        load_tab(1)
        with nc.allow_non_contiguous_dma(reason="one bias value a partition"):
            nc.sync.dma_start(bias[:], br.rearrange("(m p) -> p m", p=P))
        load_wt(0, 1)
        load_wt(1, 1)
        for b in range(2):
            rows = wr[b * KP : (b + 1) * KP, :].rearrange("(B t q) n -> t B q n", t=PACK, q=8)
            for t in range(PACK):
                nc.sync.dma_start(wr_raw[b][:, t, :], rows[t])

        vecs_ps = psum.tile([P, JT], F32, name="acc")
        for b in range(2):
            nc.tensor.transpose(vecs_ps[:, b * P : (b + 1) * P], gain_rows[:, b * P : (b + 1) * P], ident[:])
        nc.vector.tensor_copy(vecs[:], vecs_ps[:, : 2 * P].rearrange("p (b c) -> p b c", b=2)[:, :, :PACK])
        gf = vecs[:].rearrange("p b t -> p (b t)")
        neg = sb("neg", [P, 8], F32)
        mag = sb("mag", [P, 8], F32)
        half_root = sb("half_root", [P, 8], F32)
        inv = sb("inv", [P, 8], F32)
        corr = sb("corr", [P, 8], F32)
        root = sb("root", [P, 8], F32)
        sgn = sb("sgn", [P, 8], F32)
        nc.vector.tensor_scalar(neg[:], gf, -1.0, SQRT_MIN, ALU.mult, ALU.max)
        nc.vector.tensor_tensor(mag[:], neg[:], gf, ALU.max)
        nc.scalar.activation(half_root[:], mag[:], ACT.Sqrt, scale=0.25)
        nc.scalar.activation(sgn[:], gf, ACT.Sign)
        nc.vector.reciprocal(inv[:], half_root[:])
        nc.vector.scalar_tensor_tensor(corr[:], mag[:], 0.25, inv[:], ALU.mult, ALU.mult)
        nc.vector.tensor_tensor(root[:], corr[:], half_root[:], ALU.add)

        def gather(name, window, dtype, offsets, cols, offset=None):
            n = (cols.stop - cols.start) * 16
            if offset is None:
                dst = sb(name, [P, n], dtype)
            else:
                dst = reuse.tile([P, n], dtype, name=name, align_bytes=64, offset=offset)
            nc.vector.tensor_copy(dst[:], window[:].bitcast(dtype).indirect(offsets[:, cols]))
            return dst

        halves = [slice(0, JT // 16), slice(JT // 16, 2 * JT // 16)]
        whole = slice(0, S // 16)

        def quantize(name, src, width):
            codes = sb(name + "_c", [P, width], U32)
            scales = sb(name + "_s", [P, width], U8)
            nc.vector.quantize_mx(out=codes[:].bitcast(FP8X4), scales=scales[:], in_=src)
            return codes, scales

        wt_bf = {}
        wtq = {}

        def round_wt(a, b, engine):
            if b == 0:
                dst = sb("wt_bf%d%d" % (a, b), [P, KP * PACK], BF16)
            else:
                dst = late_bf16("wt_bf%d%d" % (a, b), [P, KP * PACK], 0)
            o = dst[:].rearrange("p (t B q i) -> p B t q i", t=PACK, q=8, i=PACK)
            s = wt_raw[a, b][:].rearrange("p i (B t q) -> p B t q i", t=PACK, q=8)
            if engine[0] == "s":
                nc.scalar.copy(o, s)
            else:
                nc.vector.tensor_copy(o, s)
            wt_bf[a, b] = dst

        def quant_wt(a, b):
            wtq[a, b] = quantize("wtq%d%d" % (a, b), wt_bf[a, b][:], KP)

        v2_w = [gather("v2_w%d" % j, tab2_w, U32, list2, halves[j]) for j in range(2)]
        ws_w = sb("ws_w", [P, H // 2], I32)
        ws_sc = sb("ws_sc", [P, H // 4], I32)
        for b in range(2):
            nc.vector.tensor_copy(
                ws_w[:, b * 256 : (b + 1) * 256].rearrange("p (t B w) -> p B t w", t=PACK, w=4),
                ws_w_raw[:, b * 256 : (b + 1) * 256].rearrange("p (B t w) -> p B t w", t=PACK, w=4),
            )
        v2_s = gather("v2_s", tab2_sc, U8, list2, whole)
        for b in range(2):
            nc.vector.tensor_copy(
                ws_sc[:, b * 128 : (b + 1) * 128].rearrange("p (t B w) -> p B t w", t=PACK, w=2),
                ws_sc_raw[:, b * 128 : (b + 1) * 128].rearrange("p (B t w) -> p B t w", t=PACK, w=2),
            )
        v_s = gather("v_s", tab_sc, U8, list1, whole)
        round_wt(0, 0, "ssss")
        round_wt(1, 0, "ssss")
        quant_wt(0, 0)
        quant_wt(1, 0)
        v_w = {}
        for j in range(2):
            v_w[0, j] = gather("v_w0%d" % j, tab_w[0], U32, list1, halves[j], 4 * T + 4 * JT * j)

        x = {}

        def pass_ws(b, j):
            for t in range(PACK):
                x[b, j, t] = psum.tile([P, JT], F32, name="acc")
                c = b * KP + t * P
                nc.tensor.matmul_mx(
                    x[b, j, t][:],
                    lhsT=ws_w[:].bitcast(U8)[:, 2 * c : 2 * (c + P)].bitcast(FP4X4),
                    lhsT_scale=ws_sc[:].bitcast(U8)[:, c : c + P],
                    rhs=v2_w[j][:].bitcast(FP8X4),
                    rhs_scale=v2_s[:, j * JT : (j + 1) * JT],
                    start=True,
                    stop=False,
                )

        def pass_wt(a, b, j):
            codes, scales = wtq[a, b]
            for t in range(PACK):
                nc.tensor.matmul_mx(
                    x[b, j, t][:],
                    lhsT=codes[:, t * P : (t + 1) * P].bitcast(FP8X4),
                    lhsT_scale=scales[:, t * P : (t + 1) * P],
                    rhs=v_w[a, j][:].bitcast(FP8X4),
                    rhs_scale=v_s[4 + 4 * a :, j * JT : (j + 1) * JT],
                    start=False,
                    stop=(a == 1),
                )

        r = {}
        hb = {}
        hq = {}

        def relu(b, j, t, engine):
            if (b, j) not in r:
                r[b, j] = sb("r%d%d" % (b, j), [P, PACK, JT], F32)
            sc = root[:, b * PACK + t : b * PACK + t + 1]
            if engine == "s":
                nc.scalar.activation(r[b, j][:, t, :], x[b, j, t][:], ACT.Relu, scale=sc)
            else:
                nc.vector.tensor_scalar(r[b, j][:, t, :], x[b, j, t][:], sc, 0.0, ALU.mult, ALU.max)

        def square(b, j, engine, lo, hi):
            if (b, j) not in hb:
                hb[b, j] = sb("hb%d%d" % (b, j), [P, JT, PACK], BF16)
            src = r[b, j][:, :, lo:hi].rearrange("p t c -> p c t")
            dst = hb[b, j][:, lo:hi, :]
            if engine == "s":
                nc.scalar.activation(dst, src, ACT.Square)
            else:
                nc.vector.tensor_tensor(dst, src, src, ALU.mult)

        def quant_h(b, j):
            hq[b, j] = quantize("hq%d%d" % (b, j), hb[b, j][:].rearrange("p c t -> p (c t)"), JT)

        wr_bf = {}
        wrq = {}

        def round_wr(b, lo, hi):
            if b not in wr_bf:
                wr_bf[b] = late_bf16("wr_bf%d" % b, [P, N, PACK], 0)
            nc.vector.tensor_tensor(
                wr_bf[b][:, lo:hi, :],
                wr_raw[b][:, :, lo:hi].rearrange("p t c -> p c t"),
                sgn[:, b * PACK : (b + 1) * PACK].unsqueeze(1).to_broadcast([P, hi - lo, PACK]),
                ALU.mult,
            )

        def quant_wr(b):
            wrq[b] = quantize("wrq%d" % b, wr_bf[b][:].rearrange("p n t -> p (n t)"), N)

        y = {}

        def pass_wr(b, j):
            codes, scales = wrq[b]
            for m in range(N // P):
                if b == 0:
                    y[j, m] = psum.tile([P, JT], F32, name="acc")
                nc.tensor.matmul_mx(
                    y[j, m][:],
                    lhsT=codes[:, m * P : (m + 1) * P].bitcast(FP8X4),
                    lhsT_scale=scales[:, m * P : (m + 1) * P],
                    rhs=hq[b, j][0][:].bitcast(FP8X4),
                    rhs_scale=hq[b, j][1][:],
                    start=(b == 0),
                    stop=(b == 1),
                )

        def finish(j, m, engine):
            res = sb("res%d%d" % (j, m), [P, JT], F32)
            if engine == "s":
                nc.scalar.activation(res[:], y[j, m][:], ACT.Identity, bias=bias[:, m : m + 1])
            else:
                nc.vector.tensor_scalar(res[:], y[j, m][:], bias[:, m : m + 1], None, ALU.add)
            nc.sync.dma_start(out[m * P : (m + 1) * P, j * JT : (j + 1) * JT], res[:])

        pass_ws(0, 0)
        pass_ws(0, 1)
        pass_wt(0, 0, 0)
        pass_wt(0, 0, 1)
        for j in range(2):
            v_w[1, j] = gather("v_w1%d" % j, tab_w[1], U32, list1, halves[j])
            pass_wt(1, 0, j)
        relu(0, 0, 0, "s")
        relu(0, 0, 1, "s")
        relu(0, 0, 2, "s")
        relu(0, 0, 3, "s")
        round_wt(0, 1, "vvvv")
        relu(0, 1, 0, "s")
        relu(0, 1, 1, "s")
        relu(0, 1, 2, "s")
        relu(0, 1, 3, "v")
        quant_wt(0, 1)
        pass_ws(1, 0)
        pass_wt(0, 1, 0)
        round_wt(1, 1, "vvvv")
        pass_ws(1, 1)
        pass_wt(0, 1, 1)
        quant_wt(1, 1)
        pass_wt(1, 1, 0)
        pass_wt(1, 1, 1)
        square(0, 0, "s", 0, 256)
        square(0, 0, "s", 256, 512)
        round_wr(0, 0, 256)
        round_wr(0, 256, 512)
        relu(1, 0, 0, "s")
        relu(1, 0, 1, "s")
        relu(1, 0, 2, "s")
        relu(1, 0, 3, "s")
        quant_h(0, 0)
        quant_wr(0)
        pass_wr(0, 0)
        round_wr(1, 0, 256)
        round_wr(1, 256, 512)
        square(1, 0, "s", 0, 256)
        square(1, 0, "s", 256, 512)
        quant_wr(1)
        quant_h(1, 0)
        pass_wr(1, 0)
        relu(1, 1, 0, "s")
        relu(1, 1, 1, "s")
        relu(1, 1, 2, "s")
        relu(1, 1, 3, "s")
        square(0, 1, "v", 0, 256)
        square(0, 1, "s", 256, 512)
        quant_h(0, 1)
        pass_wr(0, 1)
        square(1, 1, "s", 0, 256)
        square(1, 1, "v", 256, 512)
        quant_h(1, 1)
        finish(0, 0, "v")
        finish(0, 1, "v")
        finish(0, 2, "s")
        finish(0, 3, "s")
        pass_wr(1, 1)
        finish(1, 0, "v")
        finish(1, 1, "s")
        finish(1, 2, "v")
        finish(1, 3, "s")
